import numpy as np
CORES = [0,1,2,3,4,5,6,7,8,9,10,11,12,13,14,15,16,17,18,19,20,21,22,23,24,25,26,27,28,29,30,31,32,33,34,35,36,37,38,39,40,41,42,43,44,45,46,47,48,49,50,51,52,53,54,55,56,57,58,59,60,61,62,63,64,65,66,67,68,69,70,71,72,73,74,75,76,77,78,79,80,81,82,83,84,85,86,87,88,89,90,91,92,93,94,95,96,97,98,99,100,101,102,103,104,105,106,107,108,109,110,111,112,113,114,115,116,117,118,119,120,121,122,123,124,125,126,127,128,129,130,131,132,133,134,135,136,137,138,139,140,141,142,143,144,145,146,147,148,149,150,151,152,153,154,155,156,157,158,159,160,161,162,163,164,165,166,167,168,169,170,171,172,173,174,175,176,177,178,179,180,181,182,183,184,185,186,187,188,189,190,191,192,193,194,195,196,197,198,199,200,201,202,203,204,205,206,207,208,209,210,211,212,213,214,215,216,217,218,219,220,221,222,223,224,225,226,227,228,229,230,231,232,233,234,235,236,237,238,239,240,241,242,243,244,245,246,247,248,249,250,251,252,253,254,255]
N = 256
PAIRS = [[16 * p + i for i in range(16)] for p in range(16)]
ACROSS = [[8 * c + (k if c % 2 == 0 else k ^ 2) for c in range(32)] for k in range(8)]
def setup_inputs(rng):
    return {"x1": rng.standard_normal((N, 128, 32), dtype=np.float32), "x2": rng.standard_normal((N, 128, 256), dtype=np.float32)}
def reference(x1, x2):
    y1 = np.empty((N, 128, 16 * 32), x1.dtype)
    for g in PAIRS:
        cat = np.concatenate([x1[r] for r in g], axis=1)
        for r in g:
            y1[r] = cat
    y2 = np.empty_like(x2)
    for g in ACROSS:
        s = x2[g].sum(axis=0, dtype=np.float64).astype(x2.dtype)
        for r in g:
            y2[r] = s
    return {"y1": y1, "y2": y2}

@@ -1,0 +1,128 @@
+from concourse.bass import DstId, RemoteDMATransfer
+
+W = 32
+SHARDS = 8
+
+SCRATCH = {
+    "xs": ("sbuf", [128, SHARDS * W], "float32"),
+    "raw": ("sbuf", [128, SHARDS * W], "float32"),
+    "two": ("sbuf", [128, 2 * W], "float32"),
+    "res": ("sbuf", [128, SHARDS * W], "float32"),
+    "cat": ("sbuf", [128, 16 * W], "float32"),
+}
+SEMAPHORES = [
+    "loaded",
+    "sent",
+    "pieces",
+    "leafsum",
+    "hostsum",
+    "done",
+    "passed",
+    "near",
+    "far",
+    "copied",
+    "stored",
+]
+
+LOW = 0x00FF
+
+
+def rank_program(g, core, T, topo):
+    rank = T.rank_of(core)
+    if rank is None:
+        return
+    S = T.sem
+    host, chip, k = topo.host(core), topo.chip(core), core % 8
+    shard, parity = chip // 2, chip % 2
+
+    def at(h, c, q):
+        return 128 * h + 8 * c + q
+
+    def blk(t, i):
+        return t[:, W * i:W * (i + 1)]
+
+    def to(d):
+        rid, pid = topo.addr(d, core)
+        return DstId(rid=rid, pnc=pid)
+
+    pair = [T.cores[r] for r in next(p for p in T.tables["PAIRS"] if rank in p)]
+
+    def slot(c):
+        return pair.index(c)
+
+    mate_chip = chip ^ 1
+    is_port = topo.may_write(core, at(host, mate_chip, k))
+    partner = at(host, chip, k ^ 2)
+    my_chip = [at(host, chip, q) for q in range(8) if q != k]
+    plane = [at(host, 2 * i + parity, k) for i in range(SHARDS)]
+    group = [T.cores[r] for r in next(a for a in T.tables["ACROSS"] if rank in a)]
+    assert all(m in group for m in plane) and at(host, mate_chip, k ^ 2) in group
+
+    sent = [0]
+
+    def call(transfers):
+        g.remote_dma_fused(transfers, local_sem=S.sent)
+
+    def move(srcs, dests, mask, sem, add=False):
+        sent[0] += bin(mask).count("1")
+        return RemoteDMATransfer(dst_ids=[to(d) for d, _ in dests], dma_engine_mask=mask, remote_sem=sem,
+                                 srcs=srcs, dsts=[ap for _, ap in dests], alu_op=1 if add else 0)
+
+    g.dma_start(T.xs[:], T.x2[:]).then_inc(S.loaded, 16)
+    g.dma_start(blk(T.cat, slot(core)), T.x1[:]).then_inc(S.loaded, 16)
+    g.wait_ge(S.loaded, 32)
+
+    others = [i for i in range(SHARDS) if i != shard]
+    first = [move([blk(T.xs, i)], [(plane[i], blk(T.raw, shard))], 1 << e, S.pieces) for e, i in enumerate(others)]
+    mine = blk(T.cat, slot(core))
+    got = [blk(T.raw, i) for i in others] + [blk(T.xs, shard)]
+
+    if not is_port:
+        first.append(move([mine], [(d, mine) for d in my_chip], 0xFF00, S.near))
+        call(first)
+
+        g.wait_ge(S.pieces, 7)
+        g.wait_ge(S.leafsum, 4)
+        g.wait_ge(S.near, 7 * 8)
+        g.wait_ge(S.far, 1 + 4)
+
+        twin = at(1 - host, chip, k ^ 2)
+        third = [move(got + [blk(T.raw, shard)], [(partner, blk(T.two, 0)), (twin, blk(T.two, 1))], LOW, S.hostsum, add=True)]
+        a = blk(T.cat, slot(at(host, mate_chip, k ^ 2)))
+        b = blk(T.cat, slot(at(host, mate_chip, k)))
+        p = blk(T.cat, slot(partner))
+        third.append(move([a], [(d, a) for d in my_chip], 0x0F00, S.copied))
+        third.append(move([b], [(d, b) for d in my_chip], 0x3000, S.copied))
+        third.append(move([p], [(at(host, chip, k ^ 2 ^ 4), p)], 0xC000, S.copied))
+        call(third)
+
+        g.wait_ge(S.copied, 3 * (4 + 2))
+        g.wait_ge(S.done, 8 * 8)
+    else:
+        over = at(host, mate_chip, k ^ 2)
+        first.append(move([mine], [(over, mine)], 1 << 7, S.far))
+        first.append(move([mine], [(d, mine) for d in my_chip if d != at(host, chip, k ^ 4)], 0xFF00, S.near))
+        call(first)
+
+        g.wait_ge(S.pieces, 7)
+        g.wait_ge(S.near, 6 * 8)
+
+        pb = blk(T.cat, slot(partner))
+        call([move(got, [(over, blk(T.raw, shard))], 0x000F, S.leafsum, add=True),
+              move([pb], [(over, pb)], 0x00F0, S.far)])
+
+        g.wait_ge(S.hostsum, 2 * 8)
+        out = blk(T.res, shard)
+        roots = [at(host, 2 * i + parity, k ^ 2) for i in range(SHARDS)]
+        call([move([blk(T.two, 0), blk(T.two, 1)], [(d, out) for d in roots + [at(host, mate_chip, k)]], LOW, S.done, add=True)])
+
+        g.wait_ge(S.done, 8)
+        call([move([out], [(plane[i], out) for i in others], LOW, S.passed)])
+
+        g.wait_ge(S.copied, 4 * (4 + 2) + 2)
+        g.wait_ge(S.passed, 7 * 8)
+
+    g.dma_start(T.y1[:], T.cat[:]).then_inc(S.stored, 16)
+    g.dma_start(T.y2[:], T.res[:]).then_inc(S.stored, 16)
+    g.wait_ge(S.stored, 32)
+    g.wait_ge(S.sent, sent[0])

@@ -4,10 +4,10 @@ W = 32
 SHARDS = 8
 
 SCRATCH = {
-    "xs": ("sbuf", [128, SHARDS * W], "float32"),
-    "raw": ("sbuf", [128, SHARDS * W], "float32"),
-    "two": ("sbuf", [128, 2 * W], "float32"),
-    "res": ("sbuf", [128, SHARDS * W], "float32"),
+    "xs": ("dram", [SHARDS, 128, W], "float32"),
+    "raw": ("dram", [SHARDS, 128, W], "float32"),
+    "two": ("dram", [2, 128, W], "float32"),
+    "res": ("dram", [SHARDS, 128, W], "float32"),
     "cat": ("sbuf", [128, 16 * W], "float32"),
 }
 SEMAPHORES = [
@@ -25,6 +25,7 @@ SEMAPHORES = [
 ]
 
 LOW = 0x00FF
+HIGH = 0xFF00
 
 
 def rank_program(g, core, T, topo):
@@ -38,20 +39,19 @@ def rank_program(g, core, T, topo):
     def at(h, c, q):
         return 128 * h + 8 * c + q
 
-    def blk(t, i):
-        return t[:, W * i:W * (i + 1)]
-
     def to(d):
         rid, pid = topo.addr(d, core)
         return DstId(rid=rid, pnc=pid)
 
     pair = [T.cores[r] for r in next(p for p in T.tables["PAIRS"] if rank in p)]
 
-    def slot(c):
-        return pair.index(c)
+    def block(c, n=1):
+        i = pair.index(c)
+        return T.cat[:, W * i:W * (i + n)]
 
     mate_chip = chip ^ 1
-    is_port = topo.may_write(core, at(host, mate_chip, k))
+    ports = [q for q in range(8) if topo.may_write(at(host, chip, q), at(host, mate_chip, q))]
+    is_port = k in ports
     partner = at(host, chip, k ^ 2)
     my_chip = [at(host, chip, q) for q in range(8) if q != k]
     plane = [at(host, 2 * i + parity, k) for i in range(SHARDS)]
@@ -69,57 +69,52 @@ def rank_program(g, core, T, topo):
                                  srcs=srcs, dsts=[ap for _, ap in dests], alu_op=1 if add else 0)
 
     g.dma_start(T.xs[:], T.x2[:]).then_inc(S.loaded, 16)
-    g.dma_start(blk(T.cat, slot(core)), T.x1[:]).then_inc(S.loaded, 16)
+    g.dma_start(block(core), T.x1[:]).then_inc(S.loaded, 16)
     g.wait_ge(S.loaded, 32)
 
     others = [i for i in range(SHARDS) if i != shard]
-    first = [move([blk(T.xs, i)], [(plane[i], blk(T.raw, shard))], 1 << e, S.pieces) for e, i in enumerate(others)]
-    mine = blk(T.cat, slot(core))
-    got = [blk(T.raw, i) for i in others] + [blk(T.xs, shard)]
+    first = [move([T.xs[i]], [(plane[i], T.raw[shard])], 1 << e, S.pieces) for e, i in enumerate(others)]
+    got = [T.raw[i] for i in others] + [T.xs[shard]]
 
     if not is_port:
-        first.append(move([mine], [(d, mine) for d in my_chip], 0xFF00, S.near))
+        first.append(move([block(core)], [(d, block(core)) for d in my_chip], HIGH, S.near))
         call(first)
 
         g.wait_ge(S.pieces, 7)
         g.wait_ge(S.leafsum, 4)
         g.wait_ge(S.near, 7 * 8)
-        g.wait_ge(S.far, 1 + 4)
+        g.wait_ge(S.far, 2 + 2)
 
         twin = at(1 - host, chip, k ^ 2)
-        third = [move(got + [blk(T.raw, shard)], [(partner, blk(T.two, 0)), (twin, blk(T.two, 1))], LOW, S.hostsum, add=True)]
-        a = blk(T.cat, slot(at(host, mate_chip, k ^ 2)))
-        b = blk(T.cat, slot(at(host, mate_chip, k)))
-        p = blk(T.cat, slot(partner))
-        third.append(move([a], [(d, a) for d in my_chip], 0x0F00, S.copied))
-        third.append(move([b], [(d, b) for d in my_chip], 0x3000, S.copied))
-        third.append(move([p], [(at(host, chip, k ^ 2 ^ 4), p)], 0xC000, S.copied))
-        call(third)
+        call([move(got + [T.raw[shard]], [(partner, T.two[0]), (twin, T.two[1])], LOW, S.hostsum, add=True),
+              move([block(partner)], [(at(host, chip, k ^ 2 ^ 4), block(partner))], HIGH, S.copied)])
+        both = block(at(host, mate_chip, 2 * ports.index(k ^ 2)), 2)
+        call([move([both], [(d, both) for d in my_chip], 0xFFFF, S.copied)])
 
-        g.wait_ge(S.copied, 3 * (4 + 2))
+        g.wait_ge(S.copied, 3 * 16)
         g.wait_ge(S.done, 8 * 8)
     else:
         over = at(host, mate_chip, k ^ 2)
-        first.append(move([mine], [(over, mine)], 1 << 7, S.far))
-        first.append(move([mine], [(d, mine) for d in my_chip if d != at(host, chip, k ^ 4)], 0xFF00, S.near))
+        first.append(move([block(core)], [(d, block(core)) for d in my_chip if d != at(host, chip, k ^ 4)], HIGH, S.near))
         call(first)
 
         g.wait_ge(S.pieces, 7)
         g.wait_ge(S.near, 6 * 8)
 
-        pb = blk(T.cat, slot(partner))
-        call([move(got, [(over, blk(T.raw, shard))], 0x000F, S.leafsum, add=True),
-              move([pb], [(over, pb)], 0x00F0, S.far)])
+        lo, hi = (block(at(host, chip, 2 * ports.index(k) + i)) for i in range(2))
+        call([move(got, [(over, T.raw[shard])], 0x000F, S.leafsum, add=True),
+              move([lo], [(over, lo)], 0x0030, S.far),
+              move([hi], [(over, hi)], 0x00C0, S.far)])
 
         g.wait_ge(S.hostsum, 2 * 8)
-        out = blk(T.res, shard)
+        out = T.res[shard]
         roots = [at(host, 2 * i + parity, k ^ 2) for i in range(SHARDS)]
-        call([move([blk(T.two, 0), blk(T.two, 1)], [(d, out) for d in roots + [at(host, mate_chip, k)]], LOW, S.done, add=True)])
+        call([move([T.two[0], T.two[1]], [(d, out) for d in roots + [at(host, mate_chip, k)]], LOW, S.done, add=True)])
 
         g.wait_ge(S.done, 8)
         call([move([out], [(plane[i], out) for i in others], LOW, S.passed)])
 
-        g.wait_ge(S.copied, 4 * (4 + 2) + 2)
+        g.wait_ge(S.copied, 4 * 16 + 8)
         g.wait_ge(S.passed, 7 * 8)
 
     g.dma_start(T.y1[:], T.cat[:]).then_inc(S.stored, 16)

from concourse.bass import DstId, RemoteDMATransfer

W = 32
SHARDS = 8

SCRATCH = {
    "xs": ("dram", [SHARDS, 128, W], "float32"),
    "raw": ("dram", [SHARDS, 128, W], "float32"),
    "two": ("dram", [2, 128, W], "float32"),
    "res": ("dram", [SHARDS, 128, W], "float32"),
    "cat": ("sbuf", [128, 16 * W], "float32"),
}
SEMAPHORES = [
    "loaded",
    "sent",
    "pieces",
    "leafsum",
    "hostsum",
    "done",
    "passed",
    "near",
    "far",
    "copied",
    "stored",
]

LOW = 0x00FF
HIGH = 0xFF00


def rank_program(g, core, T, topo):
    rank = T.rank_of(core)
    if rank is None:
        return
    S = T.sem
    host, chip, k = topo.host(core), topo.chip(core), core % 8
    shard, parity = chip // 2, chip % 2

    def at(h, c, q):
        return 128 * h + 8 * c + q

    def to(d):
        rid, pid = topo.addr(d, core)
        return DstId(rid=rid, pnc=pid)

    pair = [T.cores[r] for r in next(p for p in T.tables["PAIRS"] if rank in p)]

    def block(c, n=1):
        i = pair.index(c)
        return T.cat[:, W * i:W * (i + n)]

    mate_chip = chip ^ 1
    ports = [q for q in range(8) if topo.may_write(at(host, chip, q), at(host, mate_chip, q))]
    is_port = k in ports
    partner = at(host, chip, k ^ 2)
    my_chip = [at(host, chip, q) for q in range(8) if q != k]
    plane = [at(host, 2 * i + parity, k) for i in range(SHARDS)]
    group = [T.cores[r] for r in next(a for a in T.tables["ACROSS"] if rank in a)]
    assert all(m in group for m in plane) and at(host, mate_chip, k ^ 2) in group

    sent = [0]

    def call(transfers):
        g.remote_dma_fused(transfers, local_sem=S.sent)

    def move(srcs, dests, mask, sem, add=False):
        sent[0] += bin(mask).count("1")
        return RemoteDMATransfer(dst_ids=[to(d) for d, _ in dests], dma_engine_mask=mask, remote_sem=sem,
                                 srcs=srcs, dsts=[ap for _, ap in dests], alu_op=1 if add else 0)

    g.dma_start(T.xs[:], T.x2[:]).then_inc(S.loaded, 16)
    g.dma_start(block(core), T.x1[:]).then_inc(S.loaded, 16)
    g.wait_ge(S.loaded, 32)

    others = [i for i in range(SHARDS) if i != shard]
    first = [move([T.xs[i]], [(plane[i], T.raw[shard])], 1 << e, S.pieces) for e, i in enumerate(others)]
    got = [T.raw[i] for i in others] + [T.xs[shard]]

    if not is_port:
        first.append(move([block(core)], [(d, block(core)) for d in my_chip], HIGH, S.near))
        call(first)

        g.wait_ge(S.pieces, 7)
        g.wait_ge(S.leafsum, 4)
        g.wait_ge(S.near, 7 * 8)
        g.wait_ge(S.far, 2 + 2)

        twin = at(1 - host, chip, k ^ 2)
        call([move(got + [T.raw[shard]], [(partner, T.two[0]), (twin, T.two[1])], LOW, S.hostsum, add=True),
              move([block(partner)], [(at(host, chip, k ^ 2 ^ 4), block(partner))], HIGH, S.copied)])
        both = block(at(host, mate_chip, 2 * ports.index(k ^ 2)), 2)
        call([move([both], [(d, both) for d in my_chip], 0xFFFF, S.copied)])

        g.wait_ge(S.copied, 3 * 16)
        g.wait_ge(S.done, 8 * 8)
    else:
        over = at(host, mate_chip, k ^ 2)
        first.append(move([block(core)], [(d, block(core)) for d in my_chip if d != at(host, chip, k ^ 4)], HIGH, S.near))
        call(first)

        g.wait_ge(S.pieces, 7)
        g.wait_ge(S.near, 6 * 8)

        lo, hi = (block(at(host, chip, 2 * ports.index(k) + i)) for i in range(2))
        call([move(got, [(over, T.raw[shard])], 0x000F, S.leafsum, add=True),
              move([lo], [(over, lo)], 0x0030, S.far),
              move([hi], [(over, hi)], 0x00C0, S.far)])

        g.wait_ge(S.hostsum, 2 * 8)
        out = T.res[shard]
        roots = [at(host, 2 * i + parity, k ^ 2) for i in range(SHARDS)]
        call([move([T.two[0], T.two[1]], [(d, out) for d in roots + [at(host, mate_chip, k)]], LOW, S.done, add=True)])

        g.wait_ge(S.done, 8)
        call([move([out], [(plane[i], out) for i in others], LOW, S.passed)])

        g.wait_ge(S.copied, 4 * 16 + 8)
        g.wait_ge(S.passed, 7 * 8)

    g.dma_start(T.y1[:], T.cat[:]).then_inc(S.stored, 16)
    g.dma_start(T.y2[:], T.res[:]).then_inc(S.stored, 16)
    g.wait_ge(S.stored, 32)
    g.wait_ge(S.sent, sent[0])
